import numpy as np
import ml_dtypes


def mxq(x, axis, fmt="e4m3"):
    dtype, down = {"e4m3": (ml_dtypes.float8_e4m3fn, 7), "e5m2": (ml_dtypes.float8_e5m2, 14)}[fmt]
    v = np.moveaxis(np.asarray(x, np.float32).astype(ml_dtypes.bfloat16).astype(np.float64), axis, -1)
    blocks = v.reshape(v.shape[:-1] + (-1, 32))
    amax = np.abs(blocks).max(-1, keepdims=True)
    byte = np.maximum(np.where(amax > 0, np.frexp(amax)[1] - 1 + 127, 0) - down, 1)
    scale = np.exp2(byte - 127.0)
    codes = (blocks / scale).astype(np.float32).astype(dtype).astype(np.float64)
    return np.moveaxis((codes * scale).reshape(v.shape), -1, axis)


WIDE = False


def mx_kscale(k):
    if not WIDE:
        return np.ones(k)
    levels = np.array([10, -10, 5, -5, 0])
    if k % 512:
        return np.exp2(np.random.permutation(np.resize(levels, k // 32))).repeat(32)
    a = np.empty((k // 512, 16))
    for p in range(k // 512):
        a[p, :8] = np.random.permutation(np.resize(levels, 8))
        for g in range(8):
            far = levels[np.abs(levels - a[p, g]) >= 10]
            a[p, g + 8] = far[np.random.randint(len(far))]
    return np.exp2(a.ravel()).repeat(32)


BF16 = ml_dtypes.bfloat16


def bf(x):
    return np.asarray(x, np.float32).astype(BF16)


def f64(x):
    return np.asarray(x).astype(np.float64)


E2M1 = np.array([0.0, 0.5, 1.0, 1.5, 2.0, 3.0, 4.0, 6.0, -0.0, -0.5, -1.0, -1.5, -2.0, -3.0, -4.0, -6.0])


def pack_weight(w, fmt):
    k, n = w.shape
    w = f64(bf(w)).reshape(k // 32, 32, n)
    amax = np.abs(w).max(1)
    if fmt == "e4m3":
        byte = np.frexp(amax)[1] - 1 + 127 - 7
    else:
        mant, ex = np.frexp(amax / 6.0)
        byte = np.where(mant > 0.5, ex, ex - 1) + 127
    byte = np.clip(np.where(amax > 0, byte, 1), 1, 254)
    scaled = (w * np.exp2(127.0 - byte)[:, None, :]).reshape(k, n).astype(np.float32)
    by_word = np.ascontiguousarray(scaled.reshape(k // 512, 128, 4, n).transpose(0, 1, 3, 2))
    if fmt == "e4m3":
        words = by_word.astype(ml_dtypes.float8_e4m3fn).view(np.uint8)
    else:
        c = by_word.astype(ml_dtypes.float4_e2m1fn).view(np.uint8) & 0xF
        words = c[..., 0::2] | (c[..., 1::2] << 4)
    return np.ascontiguousarray(words), np.ascontiguousarray(byte.astype(np.uint8).reshape(k // 512, 16, n))


def unpack_weight(words, scales, fmt):
    g, p, n, _ = words.shape
    if fmt == "e4m3":
        vals = np.ascontiguousarray(words).view(ml_dtypes.float8_e4m3fn).astype(np.float64)
    else:
        nib = np.empty((g, p, n, 4), np.uint8)
        nib[..., 0::2] = words & 0xF
        nib[..., 1::2] = words >> 4
        vals = E2M1[nib]
    vals = vals * np.repeat(np.exp2(scales.astype(np.float64) - 127.0), 8, axis=1)[..., None]
    return vals.transpose(0, 1, 3, 2).reshape(g * 512, n)
def pack4(w):
    words, scales = pack_weight(w, "e2m1")
    return words.reshape(words.shape[0], 128, -1), scales


def unpack4(words, scales):
    return unpack_weight(words.reshape(words.shape[0], 128, -1, 2), scales, "e2m1")


M, X, Y, K, N = 1536, 32, 32, 1024, 1024


def setup_inputs():
    s = mx_kscale(K)
    env = np.random.standard_normal((M, K)) * s
    a1 = np.random.standard_normal((X, Y)) / np.sqrt(X)
    a2 = np.random.standard_normal((X, Y)) / np.sqrt(X)
    a3 = np.random.standard_normal((X, Y)) / np.sqrt(X)
    up_words, up_scales = pack4(np.kron(a1, a1) / s[:, None])
    mid_words, mid_scales = pack_weight(np.kron(a2, a2) / s[:, None], "e4m3")
    return {"env": bf(env),
            "up_words": up_words, "up_scales": up_scales,
            "mid_words": mid_words, "mid_scales": mid_scales,
            "down": bf(np.kron(a3, a3) / s[:, None])}


def reference(env, up_words, up_scales, mid_words, mid_scales, down):
    e = mxq(f64(env), 1, "e4m3")
    y1 = e @ unpack4(up_words, up_scales)
    y2 = e @ unpack_weight(mid_words, mid_scales, "e4m3")
    y3 = e @ mxq(f64(down), 0, "e4m3")
    y = y1 + y2 + y3
    top = np.max(y, axis=1, keepdims=True)
    return y / top

@@ -1,0 +1,283 @@
+from contextlib import ExitStack
+
+import concourse.mybir as mybir
+from concourse.masks import make_identity
+
+M, K, N = 1536, 1024, 1024
+FLOPS = 3 * 2 * M * K * N
+
+F32 = mybir.dt.float32
+BF16 = mybir.dt.bfloat16
+I32 = mybir.dt.int32
+U32 = mybir.dt.uint32
+U8 = mybir.dt.uint8
+FP8X4 = mybir.dt.float8_e4m3fn_x4
+FP4X4 = mybir.dt.float4_e2m1fn_x4
+ALU = mybir.AluOpType
+ACT = mybir.ActivationFunctionType
+
+P = 128
+PACK = 4
+K_PASS = P * PACK
+GROUPS = K // K_PASS
+HALF = 512
+HALVES = N // HALF
+TILES = M // P
+BANKS = 8
+HEAD = 4
+RUN = 4
+VECTOR_COLS = 336
+TAIL_VECTOR_COLS = 640
+
+
+def tile_environment_absorption_spin1_s10_kernel(
+    tc, env, up_words, up_scales, mid_words, mid_scales, down, out
+):
+    nc = tc.nc
+    with ExitStack() as ctx:
+        keep = ctx.enter_context(tc.tile_pool(name="keep", bufs=1))
+        work = ctx.enter_context(tc.tile_pool(name="work", bufs=4))
+        psum = ctx.enter_context(tc.psum_pool(name="psum", bufs=1))
+        ctx.enter_context(tc.manual_schedule())
+
+        bank_uses = []
+
+        def next_bank():
+            bank = psum.tile([P, HALF], F32, name="bank%d" % (len(bank_uses) % BANKS))
+            bank_uses.append(bank)
+            return bank
+
+        env_raw, env_split, env_bank, env_grouped, env_codes, env_scales = {}, {}, {}, {}, {}, {}
+        w1, w2, w3_raw, w3_grouped, w3_codes, w3_scales = {}, {}, {}, {}, {}, {}
+        acc, y, half_max, top, inv = {}, {}, {}, {}, {}
+
+        def load_env(i):
+            env_raw[i] = keep.tile([P, K], BF16, name="env_raw%d" % i, align_bytes=64)
+            nc.sync.dma_start(out=env_raw[i][:], in_=env[i * P : (i + 1) * P, :])
+
+        def load_w1(h):
+            w1[h] = keep.tile([P, GROUPS, 2 * HALF], U8, name="w1_%d" % h, align_bytes=64)
+            src = up_words.rearrange("g p b -> p g b")[:, :, 2 * HALF * h : 2 * HALF * (h + 1)]
+            nc.sync.dma_start(out=w1[h][:].bitcast(I32), in_=src.bitcast(I32))
+
+        def load_w2(h):
+            w2[h] = keep.tile([P, GROUPS, HALF], U32, name="w2_%d" % h, align_bytes=64)
+            src = mid_words.rearrange("g p n t -> p g (n t)")[:, :, PACK * HALF * h : PACK * HALF * (h + 1)]
+            nc.sync.dma_start(out=w2[h][:].bitcast(I32), in_=src.bitcast(I32))
+
+        def load_w3(g, h):
+            w3_raw[g, h] = keep.tile([P, PACK, HALF], BF16, name="w3_raw%d%d" % (g, h), align_bytes=64)
+            src = down[g * K_PASS : (g + 1) * K_PASS, h * HALF : (h + 1) * HALF]
+            nc.sync.dma_start(out=w3_raw[g, h][:], in_=src.rearrange("(p j) n -> p j n", j=PACK))
+
+        def load_scales(queue, plane, scales):
+            rows = scales.bitcast(I32).rearrange("g (q r) w -> r q g w", r=4)
+            for r in range(4):
+                dst = plane[:].bitcast(I32)[r:P:32, :].rearrange("q (g w) -> q g w", g=GROUPS)
+                queue.dma_start(out=dst, in_=rows[r])
+
+        def split_env(i):
+            env_split[i] = work.tile([P, GROUPS, 2, P], F32, name="env_split", align_bytes=64)
+            words = env_raw[i][:].bitcast(F32).rearrange("m (g p u) -> m g u p", g=GROUPS, u=2)
+            nc.scalar.copy(out=env_split[i][:], in_=words)
+
+        def transpose_env(i):
+            env_bank[i] = next_bank()
+            for g in range(GROUPS):
+                for u in range(2):
+                    if i in env_split:
+                        src = env_split[i][:, g, u, :]
+                    else:
+                        src = env_raw[i][:].bitcast(F32)[:, 2 * P * g + u : 2 * P * (g + 1) : 2]
+                    c = (2 * g + u) * P
+                    nc.tensor.transpose(env_bank[i][:, c : c + P], src, ident[:])
+
+        def group_env(i):
+            env_grouped[i] = work.tile([P, GROUPS * P * PACK], BF16, name="env_grouped", align_bytes=64)
+            nc.scalar.copy(
+                out=env_grouped[i][:].bitcast(F32).rearrange("p (g m u) -> p g m u", g=GROUPS, u=2),
+                in_=env_bank[i][:].rearrange("p (g u m) -> p g m u", g=GROUPS, u=2),
+            )
+
+        def quantize_env(i):
+            env_codes[i] = keep.tile([P, GROUPS * P], U32, name="env_codes%d" % i, align_bytes=64)
+            env_scales[i] = keep.tile([P, GROUPS * P], U8, name="env_scales%d" % i, align_bytes=64)
+            nc.vector.quantize_mx(out=env_codes[i][:].bitcast(FP8X4), scales=env_scales[i][:], in_=env_grouped[i][:])
+
+        def group_w3(g, h):
+            w3_grouped[g, h] = work.tile([P, HALF, PACK], BF16, name="w3_grouped", align_bytes=64)
+            dst = w3_grouped[g, h][:].rearrange("p (c i) t -> p c t i", i=4)
+            src = w3_raw[g, h][:].rearrange("p t (c i) -> p c t i", i=4)
+            cut = VECTOR_COLS // 4
+            nc.vector.tensor_copy(out=dst[:, :cut], in_=src[:, :cut])
+            nc.scalar.copy(out=dst[:, cut:], in_=src[:, cut:])
+
+        def quantize_w3(g, h):
+            w3_codes[g, h] = keep.tile([P, HALF], U32, name="w3_codes%d%d" % (g, h), align_bytes=64)
+            w3_scales[g, h] = keep.tile([P, HALF], U8, name="w3_scales%d%d" % (g, h), align_bytes=64)
+            nc.vector.quantize_mx(
+                out=w3_codes[g, h][:].bitcast(FP8X4),
+                scales=w3_scales[g, h][:],
+                in_=w3_grouped[g, h][:].rearrange("p n t -> p (n t)"),
+            )
+
+        def multiply(i, h, level, g):
+            first = (level, g) == (1, 0)
+            if first:
+                acc[i, h] = next_bank()
+            cols = slice(g * N + h * HALF, g * N + (h + 1) * HALF)
+            if level == 1:
+                rhs, rhs_scale = w1[h][:, g, :].bitcast(FP4X4), w1_plane[:, cols]
+            elif level == 2:
+                rhs, rhs_scale = w2[h][:, g, :].bitcast(FP8X4), w2_plane[:, cols]
+            else:
+                rhs, rhs_scale = w3_codes[g, h][:].bitcast(FP8X4), w3_scales[g, h][:]
+            nc.tensor.matmul_mx(
+                out=acc[i, h][:],
+                lhsT=env_codes[i][:, g * P : (g + 1) * P].bitcast(FP8X4),
+                lhsT_scale=env_scales[i][:, g * P : (g + 1) * P],
+                rhs=rhs,
+                rhs_scale=rhs_scale,
+                start=first,
+                stop=(level, g) == (3, GROUPS - 1),
+            )
+
+        def multiply_levels(i, h, levels):
+            for level in levels:
+                for g in range(GROUPS):
+                    multiply(i, h, level, g)
+
+        def empty_bank(i, h):
+            if h == 0:
+                y[i] = work.tile([P, N], F32, name="y", bufs=6)
+                half_max[i] = work.tile([P, 1], F32, name="half_max", bufs=6)
+                start, result = None, half_max[i]
+            else:
+                top[i] = work.tile([P, 1], F32, name="top")
+                start, result = half_max[i][:], top[i]
+            nc.vector.tensor_scalar(
+                out=y[i][:, h * HALF : (h + 1) * HALF],
+                in0=acc[i, h][:],
+                scalar1=1.0,
+                scalar2=start,
+                op0=ALU.mult,
+                op1=ALU.max,
+                accum_out=result[:],
+            )
+
+        def finish(i):
+            inv[i] = work.tile([P, 1], F32, name="inv")
+            nc.vector.reciprocal(out=inv[i][:], in_=top[i][:])
+            res = work.tile([P, N], F32, name="res")
+            rows = out[i * P : (i + 1) * P, :]
+            if i < TILES - 1:
+                nc.scalar.activation(out=res[:], in_=y[i][:], func=ACT.Copy, scale=inv[i][:])
+                nc.sync.dma_start(out=rows, in_=res[:])
+            else:
+                cut = TAIL_VECTOR_COLS
+                nc.vector.tensor_scalar(
+                    out=res[:, :cut], in0=y[i][:, :cut], scalar1=inv[i][:], scalar2=None, op0=ALU.mult
+                )
+                nc.scalar.activation(out=res[:, cut:], in_=y[i][:, cut:], func=ACT.Copy, scale=inv[i][:])
+                nc.sync.dma_start(out=rows[:, :cut], in_=res[:, :cut])
+                nc.scalar.dma_start(out=rows[:, cut:], in_=res[:, cut:])
+
+        w1_plane = keep.tile([P, GROUPS * N], U8, name="w1_plane", align_bytes=64)
+        w2_plane = keep.tile([P, GROUPS * N], U8, name="w2_plane", align_bytes=64)
+        ident = keep.tile([P, P], F32, name="ident", align_bytes=64)
+        nc.vector.memset(w1_plane[:].bitcast(I32), 0)
+        nc.vector.memset(w2_plane[:].bitcast(I32), 0)
+        make_identity(nc, ident[:])
+
+        load_env(0)
+        load_env(1)
+        load_w1(0)
+        load_scales(nc.scalar, w1_plane, up_scales)
+        load_env(2)
+        load_scales(nc.sync, w2_plane, mid_scales)
+        load_w2(0)
+        load_w3(0, 0)
+        load_env(3)
+        load_w3(1, 0)
+        load_w1(1)
+        load_w2(1)
+        load_w3(0, 1)
+        load_w3(1, 1)
+        for i in range(HEAD, TILES):
+            load_env(i)
+
+        transpose_env(0)
+        transpose_env(1)
+        group_env(0)
+        group_env(1)
+        quantize_env(0)
+        quantize_env(1)
+        multiply_levels(0, 0, [1])
+        transpose_env(2)
+        group_env(2)
+        quantize_env(2)
+        multiply_levels(1, 0, [1])
+        multiply_levels(0, 0, [2])
+        multiply_levels(1, 0, [2])
+        multiply_levels(2, 0, [1, 2])
+        group_w3(0, 0)
+        quantize_w3(0, 0)
+        transpose_env(3)
+        for i in range(3):
+            multiply(i, 0, 3, 0)
+        group_w3(1, 0)
+        group_env(3)
+        quantize_w3(1, 0)
+        quantize_env(3)
+        for i in range(3):
+            multiply(i, 0, 3, 1)
+        multiply_levels(3, 0, [1, 2, 3])
+        empty_bank(0, 0)
+        empty_bank(1, 0)
+        group_w3(0, 1)
+        quantize_w3(0, 1)
+        group_w3(1, 1)
+        quantize_w3(1, 1)
+        empty_bank(2, 0)
+        empty_bank(3, 0)
+        for i in range(2):
+            multiply_levels(i, 1, [1, 2])
+        for i in range(HEAD, HEAD + RUN):
+            split_env(i)
+        for i in range(2):
+            multiply_levels(i, 1, [3])
+        for i in range(HEAD, HEAD + RUN):
+            transpose_env(i)
+        empty_bank(0, 1)
+        finish(0)
+        empty_bank(1, 1)
+        group_env(4)
+        finish(1)
+        quantize_env(4)
+        for i in range(2, HEAD):
+            multiply_levels(i, 1, [1, 2, 3])
+            group_env(i + 3)
+            empty_bank(i, 1)
+            finish(i)
+            quantize_env(i + 3)
+        group_env(7)
+        quantize_env(7)
+
+        for i in range(HEAD, TILES):
+            if i == 6:
+                for j in range(8, TILES):
+                    transpose_env(j)
+            multiply_levels(i, 0, [1, 2, 3])
+            if i in (4, 5):
+                split_env(2 * i)
+                split_env(2 * i + 1)
+            if i in (6, 7):
+                group_env(2 * i - 4)
+                group_env(2 * i - 3)
+            empty_bank(i, 0)
+            if i in (6, 7):
+                quantize_env(2 * i - 4)
+                quantize_env(2 * i - 3)
+            multiply_levels(i, 1, [1, 2, 3])
+            empty_bank(i, 1)
+            finish(i)

@@ -24,9 +24,14 @@ HALF = 512
 HALVES = N // HALF
 TILES = M // P
 BANKS = 8
-HEAD = 4
-RUN = 4
-VECTOR_COLS = 336
+QUAD = 32
+HEAD = 5
+CHUNKS = ((5, 1), (6, 2), (8, 2), (10, 2))
+W2_ROW = 4
+PROMPT = 8
+WARM_A = 0
+WARM_B = 0
+VECTOR_COLS = (336, 288)
 TAIL_VECTOR_COLS = 640
 
 
@@ -40,14 +45,14 @@ def tile_environment_absorption_spin1_s10_kernel(
         psum = ctx.enter_context(tc.psum_pool(name="psum", bufs=1))
         ctx.enter_context(tc.manual_schedule())
 
-        bank_uses = []
+        free_banks = list(range(BANKS))
 
-        def next_bank():
-            bank = psum.tile([P, HALF], F32, name="bank%d" % (len(bank_uses) % BANKS))
-            bank_uses.append(bank)
-            return bank
+        def take_bank():
+            number = free_banks.pop(0)
+            return number, psum.tile([P, HALF], F32, name="bank%d" % number)
 
-        env_raw, env_split, env_bank, env_grouped, env_codes, env_scales = {}, {}, {}, {}, {}, {}
+        env_raw, env_bank, env_grouped, env_codes, env_scales = {}, {}, {}, {}, {}
+        quad_raw, quad_split, quad_turned, quad_grouped = {}, {}, {}, {}
         w1, w2, w3_raw, w3_grouped, w3_codes, w3_scales = {}, {}, {}, {}, {}, {}
         acc, y, half_max, top, inv = {}, {}, {}, {}, {}
 
@@ -55,60 +60,93 @@ def tile_environment_absorption_spin1_s10_kernel(
             env_raw[i] = keep.tile([P, K], BF16, name="env_raw%d" % i, align_bytes=64)
             nc.sync.dma_start(out=env_raw[i][:], in_=env[i * P : (i + 1) * P, :])
 
-        def load_w1(h):
-            w1[h] = keep.tile([P, GROUPS, 2 * HALF], U8, name="w1_%d" % h, align_bytes=64)
-            src = up_words.rearrange("g p b -> p g b")[:, :, 2 * HALF * h : 2 * HALF * (h + 1)]
-            nc.sync.dma_start(out=w1[h][:].bitcast(I32), in_=src.bitcast(I32))
+        def load_w1(g):
+            w1[g] = keep.tile([P, 2 * N], U8, name="w1_%d" % g, align_bytes=64)
+            nc.sync.dma_start(out=w1[g][:].bitcast(I32), in_=up_words[g].bitcast(I32))
 
-        def load_w2(h):
-            w2[h] = keep.tile([P, GROUPS, HALF], U32, name="w2_%d" % h, align_bytes=64)
-            src = mid_words.rearrange("g p n t -> p g (n t)")[:, :, PACK * HALF * h : PACK * HALF * (h + 1)]
-            nc.sync.dma_start(out=w2[h][:].bitcast(I32), in_=src.bitcast(I32))
+        def load_w2(g):
+            w2[g] = keep.tile([P, N], U32, name="w2_%d" % g, align_bytes=64)
+            src = mid_words[g].rearrange("p n t -> p (n t)")
+            nc.sync.dma_start(out=w2[g][:].bitcast(I32), in_=src.bitcast(I32))
 
         def load_w3(g, h):
             w3_raw[g, h] = keep.tile([P, PACK, HALF], BF16, name="w3_raw%d%d" % (g, h), align_bytes=64)
             src = down[g * K_PASS : (g + 1) * K_PASS, h * HALF : (h + 1) * HALF]
             nc.sync.dma_start(out=w3_raw[g, h][:], in_=src.rearrange("(p j) n -> p j n", j=PACK))
 
-        def load_scales(queue, plane, scales):
+        def load_scales(queue, plane, first_row, scales):
             rows = scales.bitcast(I32).rearrange("g (q r) w -> r q g w", r=4)
             for r in range(4):
-                dst = plane[:].bitcast(I32)[r:P:32, :].rearrange("q (g w) -> q g w", g=GROUPS)
+                dst = plane[:].bitcast(I32)[first_row + r : P : QUAD, :].rearrange("q (g w) -> q g w", g=GROUPS)
                 queue.dma_start(out=dst, in_=rows[r])
 
-        def split_env(i):
-            env_split[i] = work.tile([P, GROUPS, 2, P], F32, name="env_split", align_bytes=64)
-            words = env_raw[i][:].bitcast(F32).rearrange("m (g p u) -> m g u p", g=GROUPS, u=2)
-            nc.scalar.copy(out=env_split[i][:], in_=words)
-
         def transpose_env(i):
-            env_bank[i] = next_bank()
+            env_bank[i] = take_bank()
             for g in range(GROUPS):
                 for u in range(2):
-                    if i in env_split:
-                        src = env_split[i][:, g, u, :]
-                    else:
-                        src = env_raw[i][:].bitcast(F32)[:, 2 * P * g + u : 2 * P * (g + 1) : 2]
+                    src = env_raw[i][:].bitcast(F32)[:, 2 * P * g + u : 2 * P * (g + 1) : 2]
                     c = (2 * g + u) * P
-                    nc.tensor.transpose(env_bank[i][:, c : c + P], src, ident[:])
+                    nc.tensor.transpose(env_bank[i][1][:, c : c + P], src, ident[:])
 
         def group_env(i):
+            number, bank = env_bank[i]
             env_grouped[i] = work.tile([P, GROUPS * P * PACK], BF16, name="env_grouped", align_bytes=64)
             nc.scalar.copy(
                 out=env_grouped[i][:].bitcast(F32).rearrange("p (g m u) -> p g m u", g=GROUPS, u=2),
-                in_=env_bank[i][:].rearrange("p (g u m) -> p g m u", g=GROUPS, u=2),
+                in_=bank[:].rearrange("p (g u m) -> p g m u", g=GROUPS, u=2),
             )
+            free_banks.append(number)
 
         def quantize_env(i):
-            env_codes[i] = keep.tile([P, GROUPS * P], U32, name="env_codes%d" % i, align_bytes=64)
-            env_scales[i] = keep.tile([P, GROUPS * P], U8, name="env_scales%d" % i, align_bytes=64)
-            nc.vector.quantize_mx(out=env_codes[i][:].bitcast(FP8X4), scales=env_scales[i][:], in_=env_grouped[i][:])
+            codes = keep.tile([P, GROUPS * P], U32, name="env_codes%d" % i, align_bytes=64)
+            scales = keep.tile([P, GROUPS * P], U8, name="env_scales%d" % i, align_bytes=64)
+            nc.vector.quantize_mx(out=codes[:].bitcast(FP8X4), scales=scales[:], in_=env_grouped[i][:])
+            for g in range(GROUPS):
+                env_codes[i, g], env_scales[i, g] = codes[:, g * P : (g + 1) * P], scales[:, g * P : (g + 1) * P]
+
+        def load_quads(c, g):
+            first, count = CHUNKS[c]
+            quad_raw[c, g] = keep.tile([P, count * P // QUAD, P], BF16, name="quad_raw%d%d" % (c, g), align_bytes=64)
+            rows = env[first * P : (first + count) * P, g * K_PASS : (g + 1) * K_PASS]
+            src = rows.rearrange("(b r) (q k) -> q r b k", r=QUAD, k=P)
+            for q in (0, 2, 1, 3):
+                nc.sync.dma_start(out=quad_raw[c, g][q * QUAD : (q + 1) * QUAD], in_=src[q])
+
+        def split_quads(c, g):
+            words = CHUNKS[c][1] * 2 * P
+            quad_split[c, g] = work.tile([P, words], F32, name="quad_split", align_bytes=64, bufs=3)
+            nc.scalar.copy(
+                out=quad_split[c, g][:].rearrange("p (b u s) -> p b u s", u=2, s=QUAD),
+                in_=quad_raw[c, g][:].bitcast(F32).rearrange("p b (s u) -> p b u s", u=2),
+            )
+
+        def turn_quads(c, g):
+            words = CHUNKS[c][1] * 2 * P
+            quad_turned[c, g] = work.tile([P, words], F32, name="quad_turned", align_bytes=64, bufs=3)
+            nc.vector.transpose(out=quad_turned[c, g][:], in_=quad_split[c, g][:])
+
+        def group_quads(c, g):
+            rows = CHUNKS[c][1] * P
+            quad_grouped[c, g] = work.tile([P, rows * PACK], BF16, name="quad_grouped", align_bytes=64, bufs=3)
+            nc.scalar.copy(
+                out=quad_grouped[c, g][:].bitcast(F32).rearrange("p (b r u) -> p b r u", u=2, r=QUAD),
+                in_=quad_turned[c, g][:].rearrange("p (b u r) -> p b r u", u=2, r=QUAD),
+            )
+
+        def quantize_quads(c, g):
+            first, count = CHUNKS[c]
+            codes = keep.tile([P, count * P], U32, name="quad_codes%d%d" % (c, g), align_bytes=64)
+            scales = keep.tile([P, count * P], U8, name="quad_scales%d%d" % (c, g), align_bytes=64)
+            nc.vector.quantize_mx(out=codes[:].bitcast(FP8X4), scales=scales[:], in_=quad_grouped[c, g][:])
+            for j in range(count):
+                cols = slice(j * P, (j + 1) * P)
+                env_codes[first + j, g], env_scales[first + j, g] = codes[:, cols], scales[:, cols]
 
         def group_w3(g, h):
             w3_grouped[g, h] = work.tile([P, HALF, PACK], BF16, name="w3_grouped", align_bytes=64)
             dst = w3_grouped[g, h][:].rearrange("p (c i) t -> p c t i", i=4)
             src = w3_raw[g, h][:].rearrange("p t (c i) -> p c t i", i=4)
-            cut = VECTOR_COLS // 4
+            cut = VECTOR_COLS[h] // 4
             nc.vector.tensor_copy(out=dst[:, :cut], in_=src[:, :cut])
             nc.scalar.copy(out=dst[:, cut:], in_=src[:, cut:])
 
@@ -124,18 +162,18 @@ def tile_environment_absorption_spin1_s10_kernel(
         def multiply(i, h, level, g):
             first = (level, g) == (1, 0)
             if first:
-                acc[i, h] = next_bank()
+                acc[i, h] = take_bank()
             cols = slice(g * N + h * HALF, g * N + (h + 1) * HALF)
             if level == 1:
-                rhs, rhs_scale = w1[h][:, g, :].bitcast(FP4X4), w1_plane[:, cols]
+                rhs, rhs_scale = w1[g][:, 2 * HALF * h : 2 * HALF * (h + 1)].bitcast(FP4X4), w1_plane[:, cols]
             elif level == 2:
-                rhs, rhs_scale = w2[h][:, g, :].bitcast(FP8X4), w2_plane[:, cols]
+                rhs, rhs_scale = w2[g][:, HALF * h : HALF * (h + 1)].bitcast(FP8X4), w2_plane[W2_ROW:, cols]
             else:
                 rhs, rhs_scale = w3_codes[g, h][:].bitcast(FP8X4), w3_scales[g, h][:]
             nc.tensor.matmul_mx(
-                out=acc[i, h][:],
-                lhsT=env_codes[i][:, g * P : (g + 1) * P].bitcast(FP8X4),
-                lhsT_scale=env_scales[i][:, g * P : (g + 1) * P],
+                out=acc[i, h][1][:],
+                lhsT=env_codes[i, g].bitcast(FP8X4),
+                lhsT_scale=env_scales[i, g],
                 rhs=rhs,
                 rhs_scale=rhs_scale,
                 start=first,
@@ -149,25 +187,28 @@ def tile_environment_absorption_spin1_s10_kernel(
 
         def empty_bank(i, h):
             if h == 0:
-                y[i] = work.tile([P, N], F32, name="y", bufs=6)
-                half_max[i] = work.tile([P, 1], F32, name="half_max", bufs=6)
+                y[i] = work.tile([P, N], F32, name="y", bufs=7)
+                half_max[i] = work.tile([P, 1], F32, name="half_max", bufs=7)
                 start, result = None, half_max[i]
             else:
                 top[i] = work.tile([P, 1], F32, name="top")
                 start, result = half_max[i][:], top[i]
             nc.vector.tensor_scalar(
                 out=y[i][:, h * HALF : (h + 1) * HALF],
-                in0=acc[i, h][:],
+                in0=acc[i, h][1][:],
                 scalar1=1.0,
                 scalar2=start,
                 op0=ALU.mult,
                 op1=ALU.max,
                 accum_out=result[:],
             )
+            free_banks.append(acc[i, h][0])
 
-        def finish(i):
+        def invert(i):
             inv[i] = work.tile([P, 1], F32, name="inv")
             nc.vector.reciprocal(out=inv[i][:], in_=top[i][:])
+
+        def scale(i):
             res = work.tile([P, N], F32, name="res")
             rows = out[i * P : (i + 1) * P, :]
             if i < TILES - 1:
@@ -191,93 +232,84 @@ def tile_environment_absorption_spin1_s10_kernel(
 
         load_env(0)
         load_env(1)
-        load_w1(0)
-        load_scales(nc.scalar, w1_plane, up_scales)
+        load_scales(nc.scalar, w1_plane, 0, up_scales)
         load_env(2)
-        load_scales(nc.sync, w2_plane, mid_scales)
-        load_w2(0)
-        load_w3(0, 0)
-        load_env(3)
-        load_w3(1, 0)
+        load_w1(0)
         load_w1(1)
+        load_scales(nc.sync, w2_plane, W2_ROW, mid_scales)
+        load_w2(0)
         load_w2(1)
+        load_w3(0, 0)
+        load_w3(1, 0)
+        load_env(3)
+        load_env(4)
         load_w3(0, 1)
         load_w3(1, 1)
-        for i in range(HEAD, TILES):
-            load_env(i)
+        for c in range(len(CHUNKS)):
+            for g in range(GROUPS):
+                load_quads(c, g)
 
-        transpose_env(0)
-        transpose_env(1)
-        group_env(0)
-        group_env(1)
-        quantize_env(0)
-        quantize_env(1)
-        multiply_levels(0, 0, [1])
-        transpose_env(2)
-        group_env(2)
-        quantize_env(2)
-        multiply_levels(1, 0, [1])
-        multiply_levels(0, 0, [2])
-        multiply_levels(1, 0, [2])
-        multiply_levels(2, 0, [1, 2])
+        for i in range(3):
+            transpose_env(i)
+            group_env(i)
+            quantize_env(i)
+        for level in (1, 2):
+            for g in range(GROUPS):
+                for i in range(3):
+                    for h in range(HALVES):
+                        multiply(i, h, level, g)
         group_w3(0, 0)
         quantize_w3(0, 0)
+        group_w3(1, 0)
+        quantize_w3(1, 0)
         transpose_env(3)
+        transpose_env(4)
         for i in range(3):
             multiply(i, 0, 3, 0)
-        group_w3(1, 0)
-        group_env(3)
-        quantize_w3(1, 0)
-        quantize_env(3)
         for i in range(3):
             multiply(i, 0, 3, 1)
+        group_env(3)
+        quantize_env(3)
+        group_env(4)
+        quantize_env(4)
         multiply_levels(3, 0, [1, 2, 3])
-        empty_bank(0, 0)
-        empty_bank(1, 0)
+        multiply_levels(4, 0, [1, 2, 3])
+        units = [(c, g) for c in range(len(CHUNKS)) for g in range(GROUPS)]
         group_w3(0, 1)
+        empty_bank(0, 0)
         quantize_w3(0, 1)
         group_w3(1, 1)
         quantize_w3(1, 1)
+        split_quads(*units[0])
+        split_quads(*units[1])
+        empty_bank(1, 0)
+        split_quads(*units[2])
+        for unit in units[:3]:
+            turn_quads(*unit)
+            group_quads(*unit)
+        split_quads(*units[3])
         empty_bank(2, 0)
+        quantize_quads(*units[0])
+        quantize_quads(*units[1])
         empty_bank(3, 0)
-        for i in range(2):
-            multiply_levels(i, 1, [1, 2])
-        for i in range(HEAD, HEAD + RUN):
-            split_env(i)
-        for i in range(2):
-            multiply_levels(i, 1, [3])
-        for i in range(HEAD, HEAD + RUN):
-            transpose_env(i)
-        empty_bank(0, 1)
-        finish(0)
-        empty_bank(1, 1)
-        group_env(4)
-        finish(1)
-        quantize_env(4)
-        for i in range(2, HEAD):
-            multiply_levels(i, 1, [1, 2, 3])
-            group_env(i + 3)
-            empty_bank(i, 1)
-            finish(i)
-            quantize_env(i + 3)
-        group_env(7)
-        quantize_env(7)
+        empty_bank(4, 0)
 
-        for i in range(HEAD, TILES):
-            if i == 6:
-                for j in range(8, TILES):
-                    transpose_env(j)
-            multiply_levels(i, 0, [1, 2, 3])
-            if i in (4, 5):
-                split_env(2 * i)
-                split_env(2 * i + 1)
-            if i in (6, 7):
-                group_env(2 * i - 4)
-                group_env(2 * i - 3)
-            empty_bank(i, 0)
-            if i in (6, 7):
-                quantize_env(2 * i - 4)
-                quantize_env(2 * i - 3)
-            multiply_levels(i, 1, [1, 2, 3])
+        for i in range(TILES):
+            multiply_levels(i, 1, [3] if i < 3 else [1, 2, 3])
+            if i + 4 < len(units):
+                split_quads(*units[i + 4])
+            if i + 3 < len(units):
+                turn_quads(*units[i + 3])
+                group_quads(*units[i + 3])
             empty_bank(i, 1)
-            finish(i)
+            if i + 2 < len(units):
+                quantize_quads(*units[i + 2])
+            if i >= PROMPT or i + 1 < HEAD:
+                invert(i)
+                scale(i)
+            if HEAD <= i + 1 < TILES:
+                multiply_levels(i + 1, 0, [1, 2, 3])
+                empty_bank(i + 1, 0)
+                if i < PROMPT:
+                    invert(i)
+                    scale(i)

@@ -29,8 +29,8 @@ HEAD = 5
 CHUNKS = ((5, 1), (6, 2), (8, 2), (10, 2))
 W2_ROW = 4
 PROMPT = 8
-WARM_A = 0
-WARM_B = 0
+WARM_A = 5
+WARM_B = 2
 VECTOR_COLS = (336, 288)
 TAIL_VECTOR_COLS = 640
 
@@ -223,6 +223,14 @@ def tile_environment_absorption_spin1_s10_kernel(
                 nc.sync.dma_start(out=rows[:, :cut], in_=res[:, :cut])
                 nc.scalar.dma_start(out=rows[:, cut:], in_=res[:, cut:])
 
+        def warm(count):
+            number, bank = take_bank()
+            for j in range(count):
+                nc.tensor.matmul(bank[:], lhsT=zeros[:, :P], rhs=zeros[:], start=True, stop=True)
+            free_banks.append(number)
+
+        zeros = keep.tile([P, HALF], BF16, name="zeros", align_bytes=64)
+        nc.vector.memset(zeros[:], 0.0)
         w1_plane = keep.tile([P, GROUPS * N], U8, name="w1_plane", align_bytes=64)
         w2_plane = keep.tile([P, GROUPS * N], U8, name="w2_plane", align_bytes=64)
         ident = keep.tile([P, P], F32, name="ident", align_bytes=64)
@@ -249,8 +257,11 @@ def tile_environment_absorption_spin1_s10_kernel(
             for g in range(GROUPS):
                 load_quads(c, g)
 
+        warm(WARM_A)
         for i in range(3):
             transpose_env(i)
+            if i == 1:
+                warm(WARM_B)
             group_env(i)
             quantize_env(i)
         for level in (1, 2):

@@ -31,7 +31,7 @@ W2_ROW = 4
 PROMPT = 8
 WARM_A = 5
 WARM_B = 2
-VECTOR_COLS = (336, 288)
+VECTOR_COLS = (256, 256)
 TAIL_VECTOR_COLS = 640
 
 
@@ -52,6 +52,7 @@ def tile_environment_absorption_spin1_s10_kernel(
             return number, psum.tile([P, HALF], F32, name="bank%d" % number)
 
         env_raw, env_bank, env_grouped, env_codes, env_scales = {}, {}, {}, {}, {}
+        env_split = {}
         quad_raw, quad_split, quad_turned, quad_grouped = {}, {}, {}, {}
         w1, w2, w3_raw, w3_grouped, w3_codes, w3_scales = {}, {}, {}, {}, {}, {}
         acc, y, half_max, top, inv = {}, {}, {}, {}, {}
@@ -69,10 +70,10 @@ def tile_environment_absorption_spin1_s10_kernel(
             src = mid_words[g].rearrange("p n t -> p (n t)")
             nc.sync.dma_start(out=w2[g][:].bitcast(I32), in_=src.bitcast(I32))
 
-        def load_w3(g, h):
-            w3_raw[g, h] = keep.tile([P, PACK, HALF], BF16, name="w3_raw%d%d" % (g, h), align_bytes=64)
-            src = down[g * K_PASS : (g + 1) * K_PASS, h * HALF : (h + 1) * HALF]
-            nc.sync.dma_start(out=w3_raw[g, h][:], in_=src.rearrange("(p j) n -> p j n", j=PACK))
+        def load_w3(g):
+            w3_raw[g] = keep.tile([P, PACK, N], BF16, name="w3_raw%d" % g, align_bytes=64)
+            src = down[g * K_PASS : (g + 1) * K_PASS, :]
+            nc.sync.dma_start(out=w3_raw[g][:], in_=src.rearrange("(p j) n -> p j n", j=PACK))
 
         def load_scales(queue, plane, first_row, scales):
             rows = scales.bitcast(I32).rearrange("g (q r) w -> r q g w", r=4)
@@ -80,11 +81,19 @@ def tile_environment_absorption_spin1_s10_kernel(
                 dst = plane[:].bitcast(I32)[first_row + r : P : QUAD, :].rearrange("q (g w) -> q g w", g=GROUPS)
                 queue.dma_start(out=dst, in_=rows[r])
 
+        def split_env(i):
+            env_split[i] = work.tile([P, GROUPS, 2, P], F32, name="env_split", align_bytes=64, bufs=2)
+            words = env_raw[i][:].bitcast(F32).rearrange("m (g p u) -> m g u p", g=GROUPS, u=2)
+            nc.scalar.copy(out=env_split[i][:], in_=words)
+
         def transpose_env(i):
             env_bank[i] = take_bank()
             for g in range(GROUPS):
                 for u in range(2):
-                    src = env_raw[i][:].bitcast(F32)[:, 2 * P * g + u : 2 * P * (g + 1) : 2]
+                    if i in env_split:
+                        src = env_split[i][:, g, u, :]
+                    else:
+                        src = env_raw[i][:].bitcast(F32)[:, 2 * P * g + u : 2 * P * (g + 1) : 2]
                     c = (2 * g + u) * P
                     nc.tensor.transpose(env_bank[i][1][:, c : c + P], src, ident[:])
 
@@ -145,7 +154,7 @@ def tile_environment_absorption_spin1_s10_kernel(
         def group_w3(g, h):
             w3_grouped[g, h] = work.tile([P, HALF, PACK], BF16, name="w3_grouped", align_bytes=64)
             dst = w3_grouped[g, h][:].rearrange("p (c i) t -> p c t i", i=4)
-            src = w3_raw[g, h][:].rearrange("p t (c i) -> p c t i", i=4)
+            src = w3_raw[g][:, :, h * HALF : (h + 1) * HALF].rearrange("p t (c i) -> p c t i", i=4)
             cut = VECTOR_COLS[h] // 4
             nc.vector.tensor_copy(out=dst[:, :cut], in_=src[:, :cut])
             nc.scalar.copy(out=dst[:, cut:], in_=src[:, cut:])
@@ -159,25 +168,49 @@ def tile_environment_absorption_spin1_s10_kernel(
                 in_=w3_grouped[g, h][:].rearrange("p n t -> p (n t)"),
             )
 
-        def multiply(i, h, level, g):
-            first = (level, g) == (1, 0)
-            if first:
-                acc[i, h] = take_bank()
-            cols = slice(g * N + h * HALF, g * N + (h + 1) * HALF)
+        def one_pass(dst, i, first_col, width, level, g):
+            h, in_half = divmod(first_col, HALF)
+            cols = slice(g * N + first_col, g * N + first_col + width)
             if level == 1:
-                rhs, rhs_scale = w1[g][:, 2 * HALF * h : 2 * HALF * (h + 1)].bitcast(FP4X4), w1_plane[:, cols]
+                rhs = w1[g][:, 2 * first_col : 2 * (first_col + width)].bitcast(FP4X4)
+                rhs_scale = w1_plane[:, cols]
             elif level == 2:
-                rhs, rhs_scale = w2[g][:, HALF * h : HALF * (h + 1)].bitcast(FP8X4), w2_plane[W2_ROW:, cols]
+                rhs = w2[g][:, first_col : first_col + width].bitcast(FP8X4)
+                rhs_scale = w2_plane[W2_ROW:, cols]
             else:
-                rhs, rhs_scale = w3_codes[g, h][:].bitcast(FP8X4), w3_scales[g, h][:]
+                rhs = w3_codes[g, h][:, in_half : in_half + width].bitcast(FP8X4)
+                rhs_scale = w3_scales[g, h][:, in_half : in_half + width]
             nc.tensor.matmul_mx(
-                out=acc[i, h][1][:],
+                out=dst,
                 lhsT=env_codes[i, g].bitcast(FP8X4),
                 lhsT_scale=env_scales[i, g],
                 rhs=rhs,
                 rhs_scale=rhs_scale,
-                start=first,
+                start=(level, g) == (1, 0),
                 stop=(level, g) == (3, GROUPS - 1),
+            )
+
+        def multiply(i, h, level, g):
+            if (level, g) == (1, 0):
+                acc[i, h] = take_bank()
+            one_pass(acc[i, h][1][:], i, h * HALF, HALF, level, g)
+
+        def last_half(i):
+            wide, narrow = take_bank()[1], take_bank()[1]
+            for first_col in range(HALF, N, P):
+                last = first_col + P == N
+                dst = narrow[:, :P] if last else wide[:, first_col - HALF : first_col - HALF + P]
+                for level in (1, 2, 3):
+                    for g in range(GROUPS):
+                        one_pass(dst, i, first_col, P, level, g)
+            wide_max = work.tile([P, 1], F32, name="wide_max")
+            top[i] = work.tile([P, 1], F32, name="top")
+            copy_with_max(y[i][:, HALF : N - P], wide[:, : HALF - P], half_max[i][:], wide_max[:])
+            copy_with_max(y[i][:, N - P :], narrow[:, :P], wide_max[:], top[i][:])
+
+        def copy_with_max(dst, src, start, result):
+            nc.vector.tensor_scalar(
+                out=dst, in0=src, scalar1=1.0, scalar2=start, op0=ALU.mult, op1=ALU.max, accum_out=result
             )
 
         def multiply_levels(i, h, levels):
@@ -193,15 +226,7 @@ def tile_environment_absorption_spin1_s10_kernel(
             else:
                 top[i] = work.tile([P, 1], F32, name="top")
                 start, result = half_max[i][:], top[i]
-            nc.vector.tensor_scalar(
-                out=y[i][:, h * HALF : (h + 1) * HALF],
-                in0=acc[i, h][1][:],
-                scalar1=1.0,
-                scalar2=start,
-                op0=ALU.mult,
-                op1=ALU.max,
-                accum_out=result[:],
-            )
+            copy_with_max(y[i][:, h * HALF : (h + 1) * HALF], acc[i, h][1][:], start, result[:])
             free_banks.append(acc[i, h][0])
 
         def invert(i):
@@ -216,12 +241,13 @@ def tile_environment_absorption_spin1_s10_kernel(
                 nc.sync.dma_start(out=rows, in_=res[:])
             else:
                 cut = TAIL_VECTOR_COLS
-                nc.vector.tensor_scalar(
-                    out=res[:, :cut], in0=y[i][:, :cut], scalar1=inv[i][:], scalar2=None, op0=ALU.mult
-                )
                 nc.scalar.activation(out=res[:, cut:], in_=y[i][:, cut:], func=ACT.Copy, scale=inv[i][:])
-                nc.sync.dma_start(out=rows[:, :cut], in_=res[:, :cut])
                 nc.scalar.dma_start(out=rows[:, cut:], in_=res[:, cut:])
+                for cols in (slice(0, cut // 2), slice(cut // 2, cut)):
+                    nc.vector.tensor_scalar(
+                        out=res[:, cols], in0=y[i][:, cols], scalar1=inv[i][:], scalar2=None, op0=ALU.mult
+                    )
+                    nc.sync.dma_start(out=rows[:, cols], in_=res[:, cols])
 
         def warm(count):
             number, bank = take_bank()
@@ -246,13 +272,11 @@ def tile_environment_absorption_spin1_s10_kernel(
         load_w1(1)
         load_scales(nc.sync, w2_plane, W2_ROW, mid_scales)
         load_w2(0)
-        load_w2(1)
-        load_w3(0, 0)
-        load_w3(1, 0)
         load_env(3)
         load_env(4)
-        load_w3(0, 1)
-        load_w3(1, 1)
+        load_w3(0)
+        load_w2(1)
+        load_w3(1)
         for c in range(len(CHUNKS)):
             for g in range(GROUPS):
                 load_quads(c, g)
@@ -264,55 +288,69 @@ def tile_environment_absorption_spin1_s10_kernel(
                 warm(WARM_B)
             group_env(i)
             quantize_env(i)
-        for level in (1, 2):
+        for tiles in ((0, 1), (2,)):
             for g in range(GROUPS):
-                for i in range(3):
+                for i in tiles:
                     for h in range(HALVES):
-                        multiply(i, h, level, g)
-        group_w3(0, 0)
-        quantize_w3(0, 0)
-        group_w3(1, 0)
-        quantize_w3(1, 0)
-        transpose_env(3)
-        transpose_env(4)
+                        multiply(i, h, 1, g)
+        split_env(3)
+        split_env(4)
         for i in range(3):
+            if i == 1:
+                transpose_env(3)
+                transpose_env(4)
+            for h in range(HALVES):
+                multiply(i, h, 2, 0)
+        for i in (3, 4):
+            group_env(i)
+            quantize_env(i)
+            multiply_levels(i, 0, [1])
+            multiply(i, 0, 2, 0)
+        for i in range(HEAD):
+            for h in range(HALVES if i < 3 else 1):
+                multiply(i, h, 2, 1)
+        for g in range(GROUPS):
+            for h in range(HALVES):
+                group_w3(g, h)
+            for h in range(HALVES):
+                quantize_w3(g, h)
+        for i in range(HEAD):
             multiply(i, 0, 3, 0)
         for i in range(3):
+            multiply(i, 1, 3, 0)
+        for i in range(HEAD):
             multiply(i, 0, 3, 1)
-        group_env(3)
-        quantize_env(3)
-        group_env(4)
-        quantize_env(4)
-        multiply_levels(3, 0, [1, 2, 3])
-        multiply_levels(4, 0, [1, 2, 3])
         units = [(c, g) for c in range(len(CHUNKS)) for g in range(GROUPS)]
-        group_w3(0, 1)
-        empty_bank(0, 0)
-        quantize_w3(0, 1)
-        group_w3(1, 1)
-        quantize_w3(1, 1)
         split_quads(*units[0])
         split_quads(*units[1])
-        empty_bank(1, 0)
         split_quads(*units[2])
-        for unit in units[:3]:
-            turn_quads(*unit)
-            group_quads(*unit)
+        for i in range(2):
+            turn_quads(*units[i])
+            group_quads(*units[i])
+            empty_bank(i, 0)
+        turn_quads(*units[2])
+        group_quads(*units[2])
         split_quads(*units[3])
-        empty_bank(2, 0)
         quantize_quads(*units[0])
         quantize_quads(*units[1])
+        empty_bank(2, 0)
         empty_bank(3, 0)
         empty_bank(4, 0)
+        for i in range(3):
+            multiply(i, 1, 3, 1)
 
         for i in range(TILES):
-            multiply_levels(i, 1, [3] if i < 3 else [1, 2, 3])
+            if 3 <= i < TILES - 1:
+                multiply_levels(i, 1, [1, 2, 3])
             if i + 4 < len(units):
                 split_quads(*units[i + 4])
             if i + 3 < len(units):
                 turn_quads(*units[i + 3])
                 group_quads(*units[i + 3])
-            empty_bank(i, 1)
+            if i < TILES - 1:
+                empty_bank(i, 1)
+            else:
+                last_half(i)
             if i + 2 < len(units):
                 quantize_quads(*units[i + 2])
             if i >= PROMPT or i + 1 < HEAD:

from contextlib import ExitStack

import concourse.mybir as mybir
from concourse.masks import make_identity

M, K, N = 1536, 1024, 1024
FLOPS = 3 * 2 * M * K * N

F32 = mybir.dt.float32
BF16 = mybir.dt.bfloat16
I32 = mybir.dt.int32
U32 = mybir.dt.uint32
U8 = mybir.dt.uint8
FP8X4 = mybir.dt.float8_e4m3fn_x4
FP4X4 = mybir.dt.float4_e2m1fn_x4
ALU = mybir.AluOpType
ACT = mybir.ActivationFunctionType

P = 128
PACK = 4
K_PASS = P * PACK
GROUPS = K // K_PASS
HALF = 512
HALVES = N // HALF
TILES = M // P
BANKS = 8
QUAD = 32
HEAD = 5
CHUNKS = ((5, 1), (6, 2), (8, 2), (10, 2))
W2_ROW = 4
PROMPT = 8
WARM_A = 5
WARM_B = 2
VECTOR_COLS = (256, 256)
TAIL_VECTOR_COLS = 640


def tile_environment_absorption_spin1_s10_kernel(
    tc, env, up_words, up_scales, mid_words, mid_scales, down, out
):
    nc = tc.nc
    with ExitStack() as ctx:
        keep = ctx.enter_context(tc.tile_pool(name="keep", bufs=1))
        work = ctx.enter_context(tc.tile_pool(name="work", bufs=4))
        psum = ctx.enter_context(tc.psum_pool(name="psum", bufs=1))
        ctx.enter_context(tc.manual_schedule())

        free_banks = list(range(BANKS))

        def take_bank():
            number = free_banks.pop(0)
            return number, psum.tile([P, HALF], F32, name="bank%d" % number)

        env_raw, env_bank, env_grouped, env_codes, env_scales = {}, {}, {}, {}, {}
        env_split = {}
        quad_raw, quad_split, quad_turned, quad_grouped = {}, {}, {}, {}
        w1, w2, w3_raw, w3_grouped, w3_codes, w3_scales = {}, {}, {}, {}, {}, {}
        acc, y, half_max, top, inv = {}, {}, {}, {}, {}

        def load_env(i):
            env_raw[i] = keep.tile([P, K], BF16, name="env_raw%d" % i, align_bytes=64)
            nc.sync.dma_start(out=env_raw[i][:], in_=env[i * P : (i + 1) * P, :])

        def load_w1(g):
            w1[g] = keep.tile([P, 2 * N], U8, name="w1_%d" % g, align_bytes=64)
            nc.sync.dma_start(out=w1[g][:].bitcast(I32), in_=up_words[g].bitcast(I32))

        def load_w2(g):
            w2[g] = keep.tile([P, N], U32, name="w2_%d" % g, align_bytes=64)
            src = mid_words[g].rearrange("p n t -> p (n t)")
            nc.sync.dma_start(out=w2[g][:].bitcast(I32), in_=src.bitcast(I32))

        def load_w3(g):
            w3_raw[g] = keep.tile([P, PACK, N], BF16, name="w3_raw%d" % g, align_bytes=64)
            src = down[g * K_PASS : (g + 1) * K_PASS, :]
            nc.sync.dma_start(out=w3_raw[g][:], in_=src.rearrange("(p j) n -> p j n", j=PACK))

        def load_scales(queue, plane, first_row, scales):
            rows = scales.bitcast(I32).rearrange("g (q r) w -> r q g w", r=4)
            for r in range(4):
                dst = plane[:].bitcast(I32)[first_row + r : P : QUAD, :].rearrange("q (g w) -> q g w", g=GROUPS)
                queue.dma_start(out=dst, in_=rows[r])

        def split_env(i):
            env_split[i] = work.tile([P, GROUPS, 2, P], F32, name="env_split", align_bytes=64, bufs=2)
            words = env_raw[i][:].bitcast(F32).rearrange("m (g p u) -> m g u p", g=GROUPS, u=2)
            nc.scalar.copy(out=env_split[i][:], in_=words)

        def transpose_env(i):
            env_bank[i] = take_bank()
            for g in range(GROUPS):
                for u in range(2):
                    if i in env_split:
                        src = env_split[i][:, g, u, :]
                    else:
                        src = env_raw[i][:].bitcast(F32)[:, 2 * P * g + u : 2 * P * (g + 1) : 2]
                    c = (2 * g + u) * P
                    nc.tensor.transpose(env_bank[i][1][:, c : c + P], src, ident[:])

        def group_env(i):
            number, bank = env_bank[i]
            env_grouped[i] = work.tile([P, GROUPS * P * PACK], BF16, name="env_grouped", align_bytes=64)
            nc.scalar.copy(
                out=env_grouped[i][:].bitcast(F32).rearrange("p (g m u) -> p g m u", g=GROUPS, u=2),
                in_=bank[:].rearrange("p (g u m) -> p g m u", g=GROUPS, u=2),
            )
            free_banks.append(number)

        def quantize_env(i):
            codes = keep.tile([P, GROUPS * P], U32, name="env_codes%d" % i, align_bytes=64)
            scales = keep.tile([P, GROUPS * P], U8, name="env_scales%d" % i, align_bytes=64)
            nc.vector.quantize_mx(out=codes[:].bitcast(FP8X4), scales=scales[:], in_=env_grouped[i][:])
            for g in range(GROUPS):
                env_codes[i, g], env_scales[i, g] = codes[:, g * P : (g + 1) * P], scales[:, g * P : (g + 1) * P]

        def load_quads(c, g):
            first, count = CHUNKS[c]
            quad_raw[c, g] = keep.tile([P, count * P // QUAD, P], BF16, name="quad_raw%d%d" % (c, g), align_bytes=64)
            rows = env[first * P : (first + count) * P, g * K_PASS : (g + 1) * K_PASS]
            src = rows.rearrange("(b r) (q k) -> q r b k", r=QUAD, k=P)
            for q in (0, 2, 1, 3):
                nc.sync.dma_start(out=quad_raw[c, g][q * QUAD : (q + 1) * QUAD], in_=src[q])

        def split_quads(c, g):
            words = CHUNKS[c][1] * 2 * P
            quad_split[c, g] = work.tile([P, words], F32, name="quad_split", align_bytes=64, bufs=3)
            nc.scalar.copy(
                out=quad_split[c, g][:].rearrange("p (b u s) -> p b u s", u=2, s=QUAD),
                in_=quad_raw[c, g][:].bitcast(F32).rearrange("p b (s u) -> p b u s", u=2),
            )

        def turn_quads(c, g):
            words = CHUNKS[c][1] * 2 * P
            quad_turned[c, g] = work.tile([P, words], F32, name="quad_turned", align_bytes=64, bufs=3)
            nc.vector.transpose(out=quad_turned[c, g][:], in_=quad_split[c, g][:])

        def group_quads(c, g):
            rows = CHUNKS[c][1] * P
            quad_grouped[c, g] = work.tile([P, rows * PACK], BF16, name="quad_grouped", align_bytes=64, bufs=3)
            nc.scalar.copy(
                out=quad_grouped[c, g][:].bitcast(F32).rearrange("p (b r u) -> p b r u", u=2, r=QUAD),
                in_=quad_turned[c, g][:].rearrange("p (b u r) -> p b r u", u=2, r=QUAD),
            )

        def quantize_quads(c, g):
            first, count = CHUNKS[c]
            codes = keep.tile([P, count * P], U32, name="quad_codes%d%d" % (c, g), align_bytes=64)
            scales = keep.tile([P, count * P], U8, name="quad_scales%d%d" % (c, g), align_bytes=64)
            nc.vector.quantize_mx(out=codes[:].bitcast(FP8X4), scales=scales[:], in_=quad_grouped[c, g][:])
            for j in range(count):
                cols = slice(j * P, (j + 1) * P)
                env_codes[first + j, g], env_scales[first + j, g] = codes[:, cols], scales[:, cols]

        def group_w3(g, h):
            w3_grouped[g, h] = work.tile([P, HALF, PACK], BF16, name="w3_grouped", align_bytes=64)
            dst = w3_grouped[g, h][:].rearrange("p (c i) t -> p c t i", i=4)
            src = w3_raw[g][:, :, h * HALF : (h + 1) * HALF].rearrange("p t (c i) -> p c t i", i=4)
            cut = VECTOR_COLS[h] // 4
            nc.vector.tensor_copy(out=dst[:, :cut], in_=src[:, :cut])
            nc.scalar.copy(out=dst[:, cut:], in_=src[:, cut:])

        def quantize_w3(g, h):
            w3_codes[g, h] = keep.tile([P, HALF], U32, name="w3_codes%d%d" % (g, h), align_bytes=64)
            w3_scales[g, h] = keep.tile([P, HALF], U8, name="w3_scales%d%d" % (g, h), align_bytes=64)
            nc.vector.quantize_mx(
                out=w3_codes[g, h][:].bitcast(FP8X4),
                scales=w3_scales[g, h][:],
                in_=w3_grouped[g, h][:].rearrange("p n t -> p (n t)"),
            )

        def one_pass(dst, i, first_col, width, level, g):
            h, in_half = divmod(first_col, HALF)
            cols = slice(g * N + first_col, g * N + first_col + width)
            if level == 1:
                rhs = w1[g][:, 2 * first_col : 2 * (first_col + width)].bitcast(FP4X4)
                rhs_scale = w1_plane[:, cols]
            elif level == 2:
                rhs = w2[g][:, first_col : first_col + width].bitcast(FP8X4)
                rhs_scale = w2_plane[W2_ROW:, cols]
            else:
                rhs = w3_codes[g, h][:, in_half : in_half + width].bitcast(FP8X4)
                rhs_scale = w3_scales[g, h][:, in_half : in_half + width]
            nc.tensor.matmul_mx(
                out=dst,
                lhsT=env_codes[i, g].bitcast(FP8X4),
                lhsT_scale=env_scales[i, g],
                rhs=rhs,
                rhs_scale=rhs_scale,
                start=(level, g) == (1, 0),
                stop=(level, g) == (3, GROUPS - 1),
            )

        def multiply(i, h, level, g):
            if (level, g) == (1, 0):
                acc[i, h] = take_bank()
            one_pass(acc[i, h][1][:], i, h * HALF, HALF, level, g)

        def last_half(i):
            wide, narrow = take_bank()[1], take_bank()[1]
            for first_col in range(HALF, N, P):
                last = first_col + P == N
                dst = narrow[:, :P] if last else wide[:, first_col - HALF : first_col - HALF + P]
                for level in (1, 2, 3):
                    for g in range(GROUPS):
                        one_pass(dst, i, first_col, P, level, g)
            wide_max = work.tile([P, 1], F32, name="wide_max")
            top[i] = work.tile([P, 1], F32, name="top")
            copy_with_max(y[i][:, HALF : N - P], wide[:, : HALF - P], half_max[i][:], wide_max[:])
            copy_with_max(y[i][:, N - P :], narrow[:, :P], wide_max[:], top[i][:])

        def copy_with_max(dst, src, start, result):
            nc.vector.tensor_scalar(
                out=dst, in0=src, scalar1=1.0, scalar2=start, op0=ALU.mult, op1=ALU.max, accum_out=result
            )

        def multiply_levels(i, h, levels):
            for level in levels:
                for g in range(GROUPS):
                    multiply(i, h, level, g)

        def empty_bank(i, h):
            if h == 0:
                y[i] = work.tile([P, N], F32, name="y", bufs=7)
                half_max[i] = work.tile([P, 1], F32, name="half_max", bufs=7)
                start, result = None, half_max[i]
            else:
                top[i] = work.tile([P, 1], F32, name="top")
                start, result = half_max[i][:], top[i]
            copy_with_max(y[i][:, h * HALF : (h + 1) * HALF], acc[i, h][1][:], start, result[:])
            free_banks.append(acc[i, h][0])

        def invert(i):
            inv[i] = work.tile([P, 1], F32, name="inv")
            nc.vector.reciprocal(out=inv[i][:], in_=top[i][:])

        def scale(i):
            res = work.tile([P, N], F32, name="res")
            rows = out[i * P : (i + 1) * P, :]
            if i < TILES - 1:
                nc.scalar.activation(out=res[:], in_=y[i][:], func=ACT.Copy, scale=inv[i][:])
                nc.sync.dma_start(out=rows, in_=res[:])
            else:
                cut = TAIL_VECTOR_COLS
                nc.scalar.activation(out=res[:, cut:], in_=y[i][:, cut:], func=ACT.Copy, scale=inv[i][:])
                nc.scalar.dma_start(out=rows[:, cut:], in_=res[:, cut:])
                for cols in (slice(0, cut // 2), slice(cut // 2, cut)):
                    nc.vector.tensor_scalar(
                        out=res[:, cols], in0=y[i][:, cols], scalar1=inv[i][:], scalar2=None, op0=ALU.mult
                    )
                    nc.sync.dma_start(out=rows[:, cols], in_=res[:, cols])

        def warm(count):
            number, bank = take_bank()
            for j in range(count):
                nc.tensor.matmul(bank[:], lhsT=zeros[:, :P], rhs=zeros[:], start=True, stop=True)
            free_banks.append(number)

        zeros = keep.tile([P, HALF], BF16, name="zeros", align_bytes=64)
        nc.vector.memset(zeros[:], 0.0)
        w1_plane = keep.tile([P, GROUPS * N], U8, name="w1_plane", align_bytes=64)
        w2_plane = keep.tile([P, GROUPS * N], U8, name="w2_plane", align_bytes=64)
        ident = keep.tile([P, P], F32, name="ident", align_bytes=64)
        nc.vector.memset(w1_plane[:].bitcast(I32), 0)
        nc.vector.memset(w2_plane[:].bitcast(I32), 0)
        make_identity(nc, ident[:])

        load_env(0)
        load_env(1)
        load_scales(nc.scalar, w1_plane, 0, up_scales)
        load_env(2)
        load_w1(0)
        load_w1(1)
        load_scales(nc.sync, w2_plane, W2_ROW, mid_scales)
        load_w2(0)
        load_env(3)
        load_env(4)
        load_w3(0)
        load_w2(1)
        load_w3(1)
        for c in range(len(CHUNKS)):
            for g in range(GROUPS):
                load_quads(c, g)

        warm(WARM_A)
        for i in range(3):
            transpose_env(i)
            if i == 1:
                warm(WARM_B)
            group_env(i)
            quantize_env(i)
        for tiles in ((0, 1), (2,)):
            for g in range(GROUPS):
                for i in tiles:
                    for h in range(HALVES):
                        multiply(i, h, 1, g)
        split_env(3)
        split_env(4)
        for i in range(3):
            if i == 1:
                transpose_env(3)
                transpose_env(4)
            for h in range(HALVES):
                multiply(i, h, 2, 0)
        for i in (3, 4):
            group_env(i)
            quantize_env(i)
            multiply_levels(i, 0, [1])
            multiply(i, 0, 2, 0)
        for i in range(HEAD):
            for h in range(HALVES if i < 3 else 1):
                multiply(i, h, 2, 1)
        for g in range(GROUPS):
            for h in range(HALVES):
                group_w3(g, h)
            for h in range(HALVES):
                quantize_w3(g, h)
        for i in range(HEAD):
            multiply(i, 0, 3, 0)
        for i in range(3):
            multiply(i, 1, 3, 0)
        for i in range(HEAD):
            multiply(i, 0, 3, 1)
        units = [(c, g) for c in range(len(CHUNKS)) for g in range(GROUPS)]
        split_quads(*units[0])
        split_quads(*units[1])
        split_quads(*units[2])
        for i in range(2):
            turn_quads(*units[i])
            group_quads(*units[i])
            empty_bank(i, 0)
        turn_quads(*units[2])
        group_quads(*units[2])
        split_quads(*units[3])
        quantize_quads(*units[0])
        quantize_quads(*units[1])
        empty_bank(2, 0)
        empty_bank(3, 0)
        empty_bank(4, 0)
        for i in range(3):
            multiply(i, 1, 3, 1)

        for i in range(TILES):
            if 3 <= i < TILES - 1:
                multiply_levels(i, 1, [1, 2, 3])
            if i + 4 < len(units):
                split_quads(*units[i + 4])
            if i + 3 < len(units):
                turn_quads(*units[i + 3])
                group_quads(*units[i + 3])
            if i < TILES - 1:
                empty_bank(i, 1)
            else:
                last_half(i)
            if i + 2 < len(units):
                quantize_quads(*units[i + 2])
            if i >= PROMPT or i + 1 < HEAD:
                invert(i)
                scale(i)
            if HEAD <= i + 1 < TILES:
                multiply_levels(i + 1, 0, [1, 2, 3])
                empty_bank(i + 1, 0)
                if i < PROMPT:
                    invert(i)
                    scale(i)
